import numpy as np, ml_dtypes
CORES = [23,119,17,113]
N = 4
import mx_ref
BF = ml_dtypes.bfloat16
def entries(a):
    return np.ascontiguousarray(a.T).reshape(-1)
def table(e):
    return np.ascontiguousarray(np.reshape(e, (-1, 16)).T).astype(np.int32)
def cols(t, e):
    v = np.concatenate([t.reshape(128, -1, 4), np.zeros((128, 1, 4), BF)], axis=1)
    return np.ascontiguousarray(v[:, e]).reshape(128, -1)
def tile(rs):
    return np.stack(rs, axis=2).reshape(128, -1).astype(BF)
def cut(t, i, w=512):
    return t[:, w * i:w * i + w]
def rowtile(v, k):
    z = np.concatenate([v, np.zeros((1, v.shape[1]), BF)])
    return np.concatenate([np.ascontiguousarray(z[k[:, 4 * m:4 * m + 4]].transpose(0, 2, 1)).reshape(128, -1) for m in range(k.shape[1] // 4)], axis=1)
def f(rng, *shape):
    return mx_ref.flush((rng.standard_normal(shape, dtype=np.float32) * np.exp2(rng.integers(-2, 3, shape[:-1] + (1,)))).astype(BF))
def wide(rng, *shape, cols=0):
    v = rng.standard_normal(shape, dtype=np.float32) * np.exp2(rng.integers(-12, 13, shape)).astype(np.float32)
    if cols: v *= np.repeat(np.exp2(rng.integers(-cols, cols + 1, shape[:-2] + (1, shape[-1] // 4))) * (rng.random(shape[:-2] + (1, shape[-1] // 4)) > 0.0625), 4, axis=-1).astype(np.float32)
    return mx_ref.flush(v.astype(BF))
T, HU, ACT = 256, 1536, 512
def lists(rng, how=None):
    a = []
    for r in range(N):
        e = rng.permutation(HU)[:ACT]
        if how == "reversed": e = np.sort(e)[::-1]
        if how == "clustered": e = rng.integers(0, HU - ACT + 1) + np.arange(ACT)
        a.append(e)
    return {"act": np.stack([e.reshape(128, 4).astype(np.int32) for e in a]), "actc": np.stack([table(e) for e in a])}
def setup_inputs(rng):
    return {"x": f(rng, N, 128, 4 * T), "w1": f(rng, N, 128, 4 * HU), "w2": f(rng, N, HU, 512), **lists(rng)}
def setup_inputs_clustered(rng):
    return {**setup_inputs(rng), **lists(rng, "clustered")}
def setup_inputs_dead(rng):
    d = setup_inputs(rng); d["x"] = np.abs(d["x"])
    for r in range(N):
        k = d["act"][r].reshape(-1)[rng.permutation(ACT)[:ACT // 2]]
        w = d["w1"][r].reshape(128, HU, 4)
        w[:, k] = -np.abs(w[:, k])
        d["w1"][r] = w.reshape(128, -1)
    return d
def setup_inputs_giant(rng):
    d = setup_inputs(rng)
    for r in range(N):
        k = d["act"][r].reshape(-1)[rng.permutation(ACT)[:ACT // 32]]
        d["w2"][r, k] = (d["w2"][r, k].astype(np.float32) * np.float32(4096)).astype(BF)
    return d
def setup_inputs_reversed(rng):
    return {**setup_inputs(rng), **lists(rng, "reversed")}
def setup_inputs_spread(rng):
    d = setup_inputs(rng); d["x"] = wide(rng, N, 128, 4 * T); d["w2"] = wide(rng, N, HU, 512); return d
def check_inputs(d):
    b = []
    for r in range(N):
        e = d["act"][r].reshape(-1)
        if e.min() < 0 or e.max() >= HU or len(set(e.tolist())) != ACT: b.append("act")
        if (entries(d["actc"][r]) != e).any(): b.append("actc")
    return b
def reference(x, w1, w2, act, actc):
    y = np.zeros((N, 128, 4 * T), np.float32)
    X = [mx_ref.quantize(x[r]) for r in range(N)]
    for s in range(N):
        A = [mx_ref.quantize(cols(w1[s], act[s][:, b])) for b in range(4)]
        rows = rowtile(w2[s], act[s])
        B = [mx_ref.quantize(np.ascontiguousarray(cut(rows, o))) for o in range(4)]
        for r in range(N):
            H = mx_ref.quantize(tile([np.maximum(mx_ref.matmul(A[b], X[r]), np.float32(0)) * np.float32(0.05) for b in range(4)]))
            for o in range(4): y[r][:, T * o:T * o + T] += mx_ref.matmul(B[o], H)
    return {"y": y}

@@ -1,0 +1,299 @@
+from concourse.bass import DstId, RemoteDMATransfer, IndirectOffsetOnAxis
+from concourse.mybir import dt, AluOpType, ActivationFunctionType
+
+CUT = 128
+F8 = "float8_e4m3fn_x4"
+SCRATCH = {
+    "idx": ("sbuf", [128, 4], "int32"),
+    "lst": ("sbuf", [128, 64], "int32"),
+    "lf": ("sbuf", [128, 128], "float32"),
+    "lt": ("sbuf", [128, 128], "float32"),
+    "off0": ("sbuf", [128, 128], "uint16"),
+    "off1": ("sbuf", [128, 128], "uint16"),
+    "off2": ("sbuf", [128, 128], "uint16"),
+    "off3": ("sbuf", [128, 128], "uint16"),
+    "xs": ("sbuf", [128, 1024], "bfloat16"),
+    "xq": ("sbuf", [128, 256], F8),
+    "xp": ("sbuf", [128, 256], "uint8"),
+    "ws": ("sbuf", [128, 6144], "bfloat16"),
+    "at": ("sbuf", [128, 2048], "bfloat16"),
+    "aq": ("sbuf", [128, 512], F8),
+    "ap": ("sbuf", [128, 512], "uint8"),
+    "rw": ("sbuf", [128, 2048], "bfloat16"),
+    "bt": ("sbuf", [128, 2048], "bfloat16"),
+    "bq": ("sbuf", [128, 512], F8),
+    "bp": ("sbuf", [128, 512], "uint8"),
+    "al": ("sbuf", [128, 1536], F8),
+    "am": ("sbuf", [128, 1536], "uint8"),
+    "bl": ("sbuf", [128, 1536], F8),
+    "bm": ("sbuf", [128, 1536], "uint8"),
+    "ht": ("sbuf", [128, 4096], "bfloat16"),
+    "hq": ("sbuf", [128, 1024], F8),
+    "hp": ("sbuf", [128, 1024], "uint8"),
+    "ys": ("sbuf", [128, 1024], "float32"),
+    "ps": ("psum", [128, 4096], "float32"),
+}
+SEMAPHORES = (["fill", "actl", "lstl", "xl", "wl", "wg", "xqd", "cp", "tr", "ofs", "bcp", "bc0", "bc1", "bc2", "qb0",
+               "qb1", "sent", "yo"]
+              + ["%s%d" % (n, i) for n in ("ga", "qa", "rw", "ym", "ye", "qh", "aa", "ax", "as", "ar", "ab", "bs", "ac")
+                 for i in range(4)]
+              + ["%s%d%d" % (n, k, b) for n in "me" for k in range(4) for b in range(4)])
+RELU = ActivationFunctionType.Relu
+COPY = ActivationFunctionType.Copy
+
+
+def rank_program(g, core, T, topo):
+    cores = T.cores
+    sem = T.sem
+
+    def slots(r):
+        c = cores[r]
+        off = [s for s in range(4) if topo.chip(cores[s]) != topo.chip(c)]
+        off.sort(key=lambda s: topo.die(cores[s]) != topo.die(c))
+        near = [s for s in range(4) if s != r and topo.chip(cores[s]) == topo.chip(c)]
+        return off + near + [r]
+
+    def helper(s):
+        c = cores[slots(s)[0]]
+        return [h for h in topo.cores_of(c) if topo.die(h) == topo.die(c) and h not in cores][0]
+
+    def dst(c):
+        rid, pid, _ = topo.addr(c)
+        return DstId(rid=rid, pnc=pid)
+
+    def codes(buf, a, b):
+        return T[buf][:, a:b].bitcast(dt.uint8)
+
+    def plane(buf, a, b):
+        return T[buf][:, a:b]
+
+    me = T.rank_of(core)
+    if me is None:
+        for s in range(4):
+            if helper(s) == core:
+                rs = slots(s)[:2]
+                es = topo.engines(core, cores[rs[0]])[::2]
+                w = len([e for e in topo.engines(cores[s], core)])
+                at = [512 * slots(r).index(s) for r in rs]
+                for name, f, buf, n in (("as", plane, "am", 512), ("ab", codes, "bl", 256)):
+                    one = sem["%s%d" % (name, s)]
+                    g.wait_ge(one, w)
+                    g.remote_dma_fused([RemoteDMATransfer(
+                        dst_ids=[dst(cores[r]) for r in rs], dma_engine_mask=sum(1 << e for e in es), remote_sem=one,
+                        srcs=[f(buf, 0, n)], dsts=[f(buf, k, k + n) for k in at])], local_sem=sem.sent)
+                g.wait_ge(sem.sent, 2 * len(es))
+        return
+
+    fa, fb, nb, _ = slots(me)
+    hc = helper(me)
+
+    far_e = topo.engines(core, cores[fa])
+    near_e = [e for e in topo.engines(core, cores[nb]) if e not in far_e]
+    even_e, odd_e = near_e[::2], near_e[1::2]
+    help_n = len(topo.engines(helper(fa), core)[::2])
+    sent = [0]
+
+    def move(es, s, f, src, to, a, b, rs):
+        sent[0] += len(es)
+        at = [512 * slots(r).index(me) for r in rs]
+        return RemoteDMATransfer(dst_ids=[dst(cores[r]) for r in rs], dma_engine_mask=sum(1 << e for e in es),
+                                 remote_sem=sem[s], srcs=[f(src, a, b)], dsts=[f(to, k + a, k + b) for k in at])
+
+    def lend(s, f, src, to, a, b):
+        sent[0] += len(far_e)
+        return RemoteDMATransfer(dst_ids=[dst(hc)], dma_engine_mask=sum(1 << e for e in far_e),
+                                 remote_sem=sem[s], srcs=[f(src, a, b)], dsts=[f(to, a, b)])
+
+    def send(ts):
+        g.remote_dma_fused(ts, local_sem=sem.sent)
+
+    V, S, P, Y = g.vector, g.scalar, g.tensor, g.sync
+
+    Y.dma_start(T.idx[:], T.act[:]).then_inc(sem.actl, 16)
+    V.memset(T.lst[:], 0).then_inc(sem.fill, 1)
+    for q, ks, a in ((Y, (0, 1), 0), (S, (2, 3), 2048)):
+        q.wait_ge(sem.fill, 1)
+        for k in ks:
+            q.dma_start(T.lst[32 * k:32 * k + 8, :], T.act[:]).then_inc(sem.lstl, 16)
+        q.dma_start(T.ws[:, a:a + 2048], T.w1[:, a:a + 2048]).then_inc(sem.wl, 16)
+    g.dma_start(T.ws[:, 4096:6144], T.w1[:, 4096:6144]).then_inc(sem.wg, 16)
+    Y.dma_start(T.xs[:], T.x[:]).then_inc(sem.xl, 16)
+
+    g.wait_ge(sem.actl, 16)
+    for t in range(4):
+        g.indirect_dma_start(T.rw[:, 512 * t:512 * t + 512], None, T.w2[:],
+                             IndirectOffsetOnAxis(ap=T.idx[:, t:t + 1], axis=0),
+                             bounds_check=1535).then_inc(sem["rw%d" % t], 16)
+    aa, ax, az, ar, ab, bz, ac = ["%s%d" % (n, me) for n in ("aa", "ax", "as", "ar", "ab", "bs", "ac")]
+    for b in (0, 1):
+        g.wait_ge(sem["qa%d" % b], 1)
+    send([move(far_e, aa, codes, "aq", "al", 0, 256, (fa,)), move(near_e, aa, codes, "aq", "al", 0, 256, (nb,))])
+    for b in (2, 3):
+        g.wait_ge(sem["qa%d" % b], 1)
+    send([lend(az, plane, "ap", "am", 0, 512), move(near_e, az, plane, "ap", "am", 0, 512, (nb,))])
+    send([move(far_e, ax, codes, "aq", "al", 256, 512, (fb,)), move(near_e, ax, codes, "aq", "al", 256, 512, (nb,))])
+    g.wait_ge(sem.qb0, 1)
+    send([lend(ab, codes, "bq", "bl", 0, 256), move(near_e, ab, codes, "bq", "bl", 0, 256, (nb,))])
+    g.wait_ge(sem.qb1, 1)
+    send([move(far_e, bz, plane, "bp", "bm", 0, 512, (fa, fb)), move(near_e, bz, plane, "bp", "bm", 0, 512, (nb,))])
+    send([move(far_e, ac, codes, "bq", "bl", 256, 512, (fa, fb))])
+    g.wait_ge(sem["aa%d" % fa], len(far_e))
+    g.wait_ge(sem["ax%d" % fb], len(far_e))
+    sent[0] += len(near_e)
+    send([RemoteDMATransfer(dst_ids=[dst(cores[nb])], dma_engine_mask=sum(1 << e for e in es), remote_sem=sem[ar],
+                            srcs=[codes("al", a, a + 256)], dsts=[codes("al", z, z + 256)])
+          for es, a, z in ((even_e, 0, 512), (odd_e, 768, 256))])
+    send([move(near_e, ac, codes, "bq", "bl", 256, 512, (nb,))])
+    g.wait_ge(sem.sent, sent[0])
+
+    V.wait_ge(sem.lstl, 64)
+    for b in range(4):
+        for d in range(2):
+            a = 32 * b + 16 * d
+            V.tensor_copy(T.lf[:, a:a + 16], T.lst[:, b:64:4]).then_inc(sem.cp, 1)
+    V.wait_ge(sem.cp, 8)
+    V.transpose(T.lt[:], T.lf[:]).then_inc(sem.tr, 1)
+    V.wait_ge(sem.tr, 1)
+    for t in range(4):
+        V.tensor_scalar(T["off%d" % t][:], T.lt[:], 4.0, float(t), AluOpType.mult, AluOpType.add).then_inc(sem.ofs, 1)
+
+    def quant_a(b):
+        V.wait_ge(sem["ga%d" % b], 4)
+        V.quantize_mx(T.aq[:, 128 * b:128 * b + 128], T.ap[:, 128 * b:128 * b + 128],
+                      T.at[:, 512 * b:512 * b + 512]).then_inc(sem["qa%d" % b], 1)
+
+    for q in (V, S):
+        q.wait_ge(sem.ofs, 4)
+        q.wait_ge(sem.wl, 32)
+        q.wait_ge(sem.wg, 16)
+    for b in range(4):
+        for t in range(4):
+            col = T.at[:, 512 * b + t:512 * b + 512:4]
+            win = T.ws[:, 0:6144].indirect(T["off%d" % t][:, 32 * b:32 * b + 8])
+            if t < (1 if b == 3 else 2):
+                V.tensor_copy(col, win).then_inc(sem["ga%d" % b], 1)
+            else:
+                S.activation(col, win, COPY).then_inc(sem["ga%d" % b], 1)
+        if b:
+            quant_a(b - 1)
+    quant_a(3)
+    V.wait_ge(sem.xl, 16)
+    V.quantize_mx(T.xq[:], T.xp[:], T.xs[:]).then_inc(sem.xqd, 1)
+
+    def relu(q, k, b, bank):
+        q.wait_ge(sem["m%d%d" % (k, b)], 1)
+        out, z = T.ht[:, 1024 * k + b:1024 * k + 1024:4], T.ps[:, 512 * bank:512 * bank + 256]
+        if q is S:
+            i = S.activation(out, z, RELU, scale=0.05)
+        else:
+            i = V.tensor_scalar(out, z, 0.0, 0.05, AluOpType.max, AluOpType.mult)
+        i.then_inc(sem["e%d%d" % (k, b)], 1)
+
+    def quant_h(k):
+        for b in range(4):
+            V.wait_ge(sem["e%d%d" % (k, b)], 1)
+        V.quantize_mx(T.hq[:, 256 * k:256 * k + 256], T.hp[:, 256 * k:256 * k + 256],
+                      T.ht[:, 1024 * k:1024 * k + 1024]).then_inc(sem["qh%d" % k], 1)
+
+    def inter(q, t, a, b, s):
+        out, rows = T.bt[:, 4 * a + t:4 * b:4], T.rw[:, 512 * t + a:512 * t + b]
+        i = S.activation(out, rows, COPY) if q is S else V.tensor_copy(out, rows)
+        i.then_inc(sem[s], 1)
+
+    for b in (0, 2):
+        relu(S, 3, b, b)
+    S.wait_ge(sem.rw3, 16)
+    inter(S, 3, CUT, 256, "bc1")
+    inter(S, 3, 256, 512, "bc2")
+    for k, b, bank in ((2, 0, 0), (2, 2, 2), (0, 1, 1), (1, 3, 3), (0, 3, 1), (1, 1, 3)):
+        relu(S, k, b, bank)
+
+    for t in range(3):
+        V.wait_ge(sem["rw%d" % t], 16)
+        inter(V, t, 0, 512, "bcp")
+    for b in (1, 3):
+        relu(V, 3, b, b)
+    quant_h(3)
+    V.wait_ge(sem.rw3, 16)
+    inter(V, 3, 0, CUT, "bc0")
+    V.wait_ge(sem.bcp, 3)
+    V.wait_ge(sem.bc0, 1)
+    V.wait_ge(sem.bc1, 1)
+    V.quantize_mx(T.bq[:, 0:256], T.bp[:, 0:256], T.bt[:, 0:1024]).then_inc(sem.qb0, 1)
+    V.wait_ge(sem.bc2, 1)
+    V.quantize_mx(T.bq[:, 256:512], T.bp[:, 256:512], T.bt[:, 1024:2048]).then_inc(sem.qb1, 1)
+    for b in (1, 3):
+        relu(V, 2, b, b)
+    quant_h(2)
+    for k, b, bank in ((0, 0, 0), (1, 2, 2), (0, 2, 0), (1, 0, 2)):
+        relu(V, k, b, bank)
+    quant_h(0)
+    quant_h(1)
+
+    def layer1(k, b, bank):
+        w, ws, a = (T.aq, T.ap, 128 * b) if k == 3 else (T.al, T.am, 512 * k + 128 * b)
+        P.matmul_mx(T.ps[:, 512 * bank:512 * bank + 256], w[:, a:a + 128], ws[:, a:a + 128],
+                    T.xq[:], T.xp[:], True, True).then_inc(sem["m%d%d" % (k, b)], 1)
+
+    def layer2(o, k, start, stop):
+        w, ws, a = (T.bq, T.bp, 128 * o) if k == 3 else (T.bl, T.bm, 512 * k + 128 * o)
+        z, c = 2048 + 512 * o, 256 * k
+        i = P.matmul_mx(T.ps[:, z:z + 256], w[:, a:a + 128], ws[:, a:a + 128],
+                        T.hq[:, c:c + 256], T.hp[:, c:c + 256], start, stop)
+        if stop:
+            i.then_inc(sem["ym%d" % o], 1)
+
+    P.wait_ge(sem.xqd, 1)
+    for b in range(4):
+        P.wait_ge(sem["qa%d" % b], 1)
+        layer1(3, b, b)
+    P.wait_ge(sem.qh3, 1)
+    P.wait_ge(sem.qb0, 1)
+    P.wait_ge(sem.qb1, 1)
+    for o in range(4):
+        layer2(o, 3, True, False)
+    for n in ("aa", "as", "ax"):
+        P.wait_ge(sem["%s%d" % (n, nb)], len(near_e))
+    for b in range(4):
+        layer1(2, b, b)
+    for k, r, n, bs in ((0, fa, "aa", (0, 1)), (1, fb, "ax", (2, 3))):
+        P.wait_ge(sem["%s%d" % (n, r)], len(far_e))
+        P.wait_ge(sem["as%d" % r], help_n)
+        for b in bs:
+            P.wait_ge(sem["e2%d" % b], 1)
+            layer1(k, b, b)
+    P.wait_ge(sem["ar%d" % nb], len(near_e))
+    for k, b, bank in ((0, 2, 0), (0, 3, 1), (1, 0, 2), (1, 1, 3)):
+        P.wait_ge(sem["e%d%d" % (bank // 2, bank)], 1)
+        layer1(k, b, bank)
+    P.wait_ge(sem.qh2, 1)
+    for n in ("ab", "bs"):
+        P.wait_ge(sem["%s%d" % (n, nb)], len(near_e))
+    for o in (0, 1):
+        layer2(o, 2, False, False)
+    for k, r in enumerate((fa, fb)):
+        P.wait_ge(sem["qh%d" % k], 1)
+        P.wait_ge(sem["bs%d" % r], len(far_e))
+        P.wait_ge(sem["ab%d" % r], help_n)
+        for o in (0, 1):
+            layer2(o, k, False, k == 1)
+    P.wait_ge(sem["ac%d" % nb], len(near_e))
+    for o in (2, 3):
+        layer2(o, 2, False, False)
+    P.wait_ge(sem["ac%d" % fa], len(far_e))
+    P.wait_ge(sem["ac%d" % fb], len(far_e))
+    for o in (2, 3):
+        layer2(o, 0, False, False)
+        layer2(o, 1, False, True)
+
+    for o in range(4):
+        a, z = 256 * o, 2048 + 512 * o
+        q = S if o % 2 else V
+        q.wait_ge(sem["ym%d" % o], 1)
+        if o % 2:
+            S.activation(T.ys[:, a:a + 256], T.ps[:, z:z + 256], COPY).then_inc(sem["ye%d" % o], 1)
+        else:
+            V.tensor_copy(T.ys[:, a:a + 256], T.ps[:, z:z + 256]).then_inc(sem["ye%d" % o], 1)
+        Y.wait_ge(sem["ye%d" % o], 1)
+        Y.dma_start(T.y[:, a:a + 256], T.ys[:, a:a + 256]).then_inc(sem.yo, 16)
+    Y.wait_ge(sem.yo, 64)

@@ -1,17 +1,13 @@
 from concourse.bass import DstId, RemoteDMATransfer, IndirectOffsetOnAxis
 from concourse.mybir import dt, AluOpType, ActivationFunctionType
 
-CUT = 128
 F8 = "float8_e4m3fn_x4"
 SCRATCH = {
     "idx": ("sbuf", [128, 4], "int32"),
-    "lst": ("sbuf", [128, 64], "int32"),
+    "lst": ("sbuf", [128, 16], "int32"),
     "lf": ("sbuf", [128, 128], "float32"),
     "lt": ("sbuf", [128, 128], "float32"),
-    "off0": ("sbuf", [128, 128], "uint16"),
-    "off1": ("sbuf", [128, 128], "uint16"),
-    "off2": ("sbuf", [128, 128], "uint16"),
-    "off3": ("sbuf", [128, 128], "uint16"),
+    "off": ("sbuf", [128, 128], "uint16"),
     "xs": ("sbuf", [128, 1024], "bfloat16"),
     "xq": ("sbuf", [128, 256], F8),
     "xp": ("sbuf", [128, 256], "uint8"),
@@ -33,10 +29,22 @@ SCRATCH = {
     "ys": ("sbuf", [128, 1024], "float32"),
     "ps": ("psum", [128, 4096], "float32"),
 }
-SEMAPHORES = (["fill", "actl", "lstl", "xl", "wl", "wg", "xqd", "cp", "tr", "ofs", "bcp", "bc0", "bc1", "bc2", "qb0",
-               "qb1", "sent", "yo"]
-              + ["%s%d" % (n, i) for n in ("ga", "qa", "rw", "ym", "ye", "qh", "aa", "ax", "as", "ar", "ab", "bs", "ac")
-                 for i in range(4)]
+CALLS = ((("A01",), (), ("A01",)),
+         (("a03",), (), ("a03",)),
+         (("A23",), (), ("A23",)),
+         (("B01",), (), ("B01",)),
+         (("b03",), (), ("b03",)),
+         ((), ("B22",), ("B22",)),
+         ((), ("B33",), ("B33",)))
+EARLY = (3,)
+GATHER_V, GATHER_S = ((0, 32), (64, 90)), ((32, 64), (90, 128))
+QUANT_A, QUANT_B = ((0, 0), (1, 1), (2, 3)), ((0, 1), (2, 3))
+TENSOR = ("130 131 132 133 120 121 122 123 230 231 232 233 100 101 110 111 102 103 112 113 "
+          "220 221 222 200 201 210 211 202 212 223 203 213").split()
+VECTOR = "3 21 23 2 00 10 02 12 0 1".split()
+SEMAPHORES = (["actl", "lstl", "xl", "wl", "wg", "xqd", "cp", "dp", "tr", "ofs", "bcp", "sent", "yo"]
+              + ["%s%d" % (n, i) for n in ("gv", "gs", "qa", "qb", "bc", "rw", "ym", "ye", "qh") for i in range(4)]
+              + ["%s%d%d" % (n, i, s) for n in "cd" for i in range(len(CALLS)) for s in range(4)]
               + ["%s%d%d" % (n, k, b) for n in "me" for k in range(4) for b in range(4)])
 RELU = ActivationFunctionType.Relu
 COPY = ActivationFunctionType.Copy
@@ -61,239 +69,217 @@ def rank_program(g, core, T, topo):
         rid, pid, _ = topo.addr(c)
         return DstId(rid=rid, pnc=pid)
 
-    def codes(buf, a, b):
-        return T[buf][:, a:b].bitcast(dt.uint8)
+    def view(piece, landed, at=0):
+        m, a, b = piece[0], at + 128 * int(piece[1]), at + 128 * int(piece[2]) + 128
+        if m.islower():
+            return T[m + ("m" if landed else "p")][:, a:b]
+        return T[m.lower() + ("l" if landed else "q")][:, a:b].bitcast(dt.uint8)
 
-    def plane(buf, a, b):
-        return T[buf][:, a:b]
+    def transfers(es, pieces, name, landed, to):
+        n = len(es) // max(len(pieces), 1)
+        return [RemoteDMATransfer(dst_ids=[dst(c) for c, _ in to],
+                                  dma_engine_mask=sum(1 << e for e in es[n * j:n * j + n]),
+                                  remote_sem=sem[name], srcs=[view(p, landed)],
+                                  dsts=[view(p, True, at) for _, at in to]) for j, p in enumerate(pieces)]
+
+    def place(r, s):
+        return cores[r], 512 * slots(r).index(s)
+
+    def shares(s, i):
+        lent, direct, near = CALLS[i]
+        far = topo.engines(cores[s], helper(s))
+        rest = [e for e in topo.engines(cores[s], cores[slots(s)[2]]) if e not in far]
+        cut = len(far) // 2 if lent and direct else len(far) * bool(lent)
+        return far[:cut], far[cut:] if direct else [], rest if near else []
 
     me = T.rank_of(core)
     if me is None:
         for s in range(4):
             if helper(s) == core:
                 rs = slots(s)[:2]
-                es = topo.engines(core, cores[rs[0]])[::2]
-                w = len([e for e in topo.engines(cores[s], core)])
-                at = [512 * slots(r).index(s) for r in rs]
-                for name, f, buf, n in (("as", plane, "am", 512), ("ab", codes, "bl", 256)):
-                    one = sem["%s%d" % (name, s)]
-                    g.wait_ge(one, w)
-                    g.remote_dma_fused([RemoteDMATransfer(
-                        dst_ids=[dst(cores[r]) for r in rs], dma_engine_mask=sum(1 << e for e in es), remote_sem=one,
-                        srcs=[f(buf, 0, n)], dsts=[f(buf, k, k + n) for k in at])], local_sem=sem.sent)
-                g.wait_ge(sem.sent, 2 * len(es))
+                es = topo.engines(core, cores[rs[0]])
+                lent = [(i, c[0]) for i, c in enumerate(CALLS) if c[0]]
+                for i, pieces in lent:
+                    name = "c%d%d" % (i, s)
+                    g.wait_ge(sem[name], len(shares(s, i)[0]))
+                    g.remote_dma_fused([x for j, r in enumerate(rs)
+                                        for x in transfers(es[j::2], pieces, name, True, [place(r, s)])],
+                                       local_sem=sem.sent)
+                g.wait_ge(sem.sent, len(lent) * len(es))
         return
 
     fa, fb, nb, _ = slots(me)
-    hc = helper(me)
-
-    far_e = topo.engines(core, cores[fa])
-    near_e = [e for e in topo.engines(core, cores[nb]) if e not in far_e]
-    even_e, odd_e = near_e[::2], near_e[1::2]
     help_n = len(topo.engines(helper(fa), core)[::2])
-    sent = [0]
-
-    def move(es, s, f, src, to, a, b, rs):
-        sent[0] += len(es)
-        at = [512 * slots(r).index(me) for r in rs]
-        return RemoteDMATransfer(dst_ids=[dst(cores[r]) for r in rs], dma_engine_mask=sum(1 << e for e in es),
-                                 remote_sem=sem[s], srcs=[f(src, a, b)], dsts=[f(to, k + a, k + b) for k in at])
-
-    def lend(s, f, src, to, a, b):
-        sent[0] += len(far_e)
-        return RemoteDMATransfer(dst_ids=[dst(hc)], dma_engine_mask=sum(1 << e for e in far_e),
-                                 remote_sem=sem[s], srcs=[f(src, a, b)], dsts=[f(to, a, b)])
-
-    def send(ts):
-        g.remote_dma_fused(ts, local_sem=sem.sent)
-
     V, S, P, Y = g.vector, g.scalar, g.tensor, g.sync
+    waited = []
+
+    def wait(q, name, n):
+        if not any(w[0] is q and w[1] == name for w in waited):
+            waited.append((q, name))
+            q.wait_ge(sem[name], n)
+
+    def made(q, piece):
+        m, a, b = piece[0].lower(), int(piece[1]), int(piece[2])
+        for j, (c, d) in enumerate(QUANT_A if m == "a" else QUANT_B):
+            if c <= b and a <= d:
+                wait(q, "q%s%d" % (m, j), 1)
+
+    def send(i):
+        lent, direct, near = CALLS[i]
+        for piece in lent + direct + near:
+            made(g, piece)
+        to_h, to_far, to_nb = shares(me, i)
+        c, d = "c%d%d" % (i, me), "d%d%d" % (i, me)
+        g.remote_dma_fused(transfers(to_h, lent, c, False, [(helper(me), 0)])
+                           + transfers(to_far, direct, d, False, [place(fa, me), place(fb, me)])
+                           + transfers(to_nb, near, c, False, [place(nb, me)]), local_sem=sem.sent)
 
     Y.dma_start(T.idx[:], T.act[:]).then_inc(sem.actl, 16)
-    V.memset(T.lst[:], 0).then_inc(sem.fill, 1)
     for q, ks, a in ((Y, (0, 1), 0), (S, (2, 3), 2048)):
-        q.wait_ge(sem.fill, 1)
         for k in ks:
-            q.dma_start(T.lst[32 * k:32 * k + 8, :], T.act[:]).then_inc(sem.lstl, 16)
+            q.dma_start(T.lst[32 * k:32 * k + 32, :], T.act[:]).then_inc(sem.lstl, 16)
         q.dma_start(T.ws[:, a:a + 2048], T.w1[:, a:a + 2048]).then_inc(sem.wl, 16)
     g.dma_start(T.ws[:, 4096:6144], T.w1[:, 4096:6144]).then_inc(sem.wg, 16)
     Y.dma_start(T.xs[:], T.x[:]).then_inc(sem.xl, 16)
 
     g.wait_ge(sem.actl, 16)
     for t in range(4):
+        for i in range(len(EARLY)):
+            if EARLY[i] == t:
+                send(i)
         g.indirect_dma_start(T.rw[:, 512 * t:512 * t + 512], None, T.w2[:],
                              IndirectOffsetOnAxis(ap=T.idx[:, t:t + 1], axis=0),
                              bounds_check=1535).then_inc(sem["rw%d" % t], 16)
-    aa, ax, az, ar, ab, bz, ac = ["%s%d" % (n, me) for n in ("aa", "ax", "as", "ar", "ab", "bs", "ac")]
-    for b in (0, 1):
-        g.wait_ge(sem["qa%d" % b], 1)
-    send([move(far_e, aa, codes, "aq", "al", 0, 256, (fa,)), move(near_e, aa, codes, "aq", "al", 0, 256, (nb,))])
-    for b in (2, 3):
-        g.wait_ge(sem["qa%d" % b], 1)
-    send([lend(az, plane, "ap", "am", 0, 512), move(near_e, az, plane, "ap", "am", 0, 512, (nb,))])
-    send([move(far_e, ax, codes, "aq", "al", 256, 512, (fb,)), move(near_e, ax, codes, "aq", "al", 256, 512, (nb,))])
-    g.wait_ge(sem.qb0, 1)
-    send([lend(ab, codes, "bq", "bl", 0, 256), move(near_e, ab, codes, "bq", "bl", 0, 256, (nb,))])
-    g.wait_ge(sem.qb1, 1)
-    send([move(far_e, bz, plane, "bp", "bm", 0, 512, (fa, fb)), move(near_e, bz, plane, "bp", "bm", 0, 512, (nb,))])
-    send([move(far_e, ac, codes, "bq", "bl", 256, 512, (fa, fb))])
-    g.wait_ge(sem["aa%d" % fa], len(far_e))
-    g.wait_ge(sem["ax%d" % fb], len(far_e))
-    sent[0] += len(near_e)
-    send([RemoteDMATransfer(dst_ids=[dst(cores[nb])], dma_engine_mask=sum(1 << e for e in es), remote_sem=sem[ar],
-                            srcs=[codes("al", a, a + 256)], dsts=[codes("al", z, z + 256)])
-          for es, a, z in ((even_e, 0, 512), (odd_e, 768, 256))])
-    send([move(near_e, ac, codes, "bq", "bl", 256, 512, (nb,))])
-    g.wait_ge(sem.sent, sent[0])
+    for i in range(len(EARLY), len(CALLS)):
+        send(i)
+    g.wait_ge(sem.sent, sum(len(es) for i in range(len(CALLS)) for es in shares(me, i)))
 
     V.wait_ge(sem.lstl, 64)
     for b in range(4):
-        for d in range(2):
-            a = 32 * b + 16 * d
-            V.tensor_copy(T.lf[:, a:a + 16], T.lst[:, b:64:4]).then_inc(sem.cp, 1)
-    V.wait_ge(sem.cp, 8)
+        for t in range(4):
+            V.tensor_scalar(T.lf[:, 32 * b + t:32 * b + 16:4], T.lst[:, b:16:4], 4.0, float(t),
+                            AluOpType.mult, AluOpType.add).then_inc(sem.cp, 1)
+    V.wait_ge(sem.cp, 16)
+    for b in range(4):
+        V.tensor_copy(T.lf[:, 32 * b + 16:32 * b + 32], T.lf[:, 32 * b:32 * b + 16]).then_inc(sem.dp, 1)
+    V.wait_ge(sem.dp, 4)
     V.transpose(T.lt[:], T.lf[:]).then_inc(sem.tr, 1)
     V.wait_ge(sem.tr, 1)
-    for t in range(4):
-        V.tensor_scalar(T["off%d" % t][:], T.lt[:], 4.0, float(t), AluOpType.mult, AluOpType.add).then_inc(sem.ofs, 1)
+    V.tensor_copy(T.off[:], T.lt[:]).then_inc(sem.ofs, 1)
 
-    def quant_a(b):
-        V.wait_ge(sem["ga%d" % b], 4)
-        V.quantize_mx(T.aq[:, 128 * b:128 * b + 128], T.ap[:, 128 * b:128 * b + 128],
-                      T.at[:, 512 * b:512 * b + 512]).then_inc(sem["qa%d" % b], 1)
+    def gather(q, j):
+        a, b = (GATHER_S if q is S else GATHER_V)[j]
+        out, win = T.at[:, 16 * a:16 * b], T.ws[:, 0:6144].indirect(T.off[:, a:b])
+        if q is S:
+            S.activation(out, win, COPY).then_inc(sem["gs%d" % j], 1)
+        else:
+            V.tensor_copy(out, win).then_inc(sem["gv%d" % j], 1)
 
     for q in (V, S):
-        q.wait_ge(sem.ofs, 4)
+        q.wait_ge(sem.ofs, 1)
         q.wait_ge(sem.wl, 32)
         q.wait_ge(sem.wg, 16)
-    for b in range(4):
-        for t in range(4):
-            col = T.at[:, 512 * b + t:512 * b + 512:4]
-            win = T.ws[:, 0:6144].indirect(T["off%d" % t][:, 32 * b:32 * b + 8])
-            if t < (1 if b == 3 else 2):
-                V.tensor_copy(col, win).then_inc(sem["ga%d" % b], 1)
-            else:
-                S.activation(col, win, COPY).then_inc(sem["ga%d" % b], 1)
-        if b:
-            quant_a(b - 1)
-    quant_a(3)
+    for j in range(len(GATHER_S)):
+        gather(S, j)
+    nxt = 0
+    for j, (c, d) in enumerate(QUANT_A):
+        a, b = 128 * c, 128 * d + 128
+        while nxt < len(GATHER_V) and GATHER_V[nxt][0] < b // 4:
+            gather(V, nxt)
+            nxt += 1
+        for name, runs in (("gv", GATHER_V), ("gs", GATHER_S)):
+            for i, (u, v) in enumerate(runs):
+                if u < b // 4 and a // 4 < v:
+                    wait(V, "%s%d" % (name, i), 1)
+        V.quantize_mx(T.aq[:, a:b], T.ap[:, a:b], T.at[:, 4 * a:4 * b]).then_inc(sem["qa%d" % j], 1)
     V.wait_ge(sem.xl, 16)
     V.quantize_mx(T.xq[:], T.xp[:], T.xs[:]).then_inc(sem.xqd, 1)
 
-    def relu(q, k, b, bank):
-        q.wait_ge(sem["m%d%d" % (k, b)], 1)
+    def inter(q, t, a, b, s):
+        out, rows = T.bt[:, 4 * a + t:4 * b:4], T.rw[:, 512 * t + a:512 * t + b]
+        q.wait_ge(sem["rw%d" % t], 16)
+        i = S.activation(out, rows, COPY) if q is S else V.tensor_copy(out, rows)
+        i.then_inc(sem[s], 1)
+
+    for t in range(3):
+        inter(V, t, 0, 512, "bcp")
+    inter(V, 3, 0, 256, "bc0")
+    V.wait_ge(sem.bcp, 3)
+    for j, (c, d) in enumerate(QUANT_B):
+        a, b = 128 * c, 128 * d + 128
+        V.wait_ge(sem["bc%d" % j], 1)
+        V.quantize_mx(T.bq[:, a:b], T.bp[:, a:b], T.bt[:, 4 * a:4 * b]).then_inc(sem["qb%d" % j], 1)
+
+    order = [w[1:] for w in TENSOR if w[0] == "1"]
+
+    def relu(q, kb):
+        k, b, bank = int(kb[0]), int(kb[1]), order.index(kb) % 4
+        q.wait_ge(sem["m" + kb], 1)
         out, z = T.ht[:, 1024 * k + b:1024 * k + 1024:4], T.ps[:, 512 * bank:512 * bank + 256]
         if q is S:
             i = S.activation(out, z, RELU, scale=0.05)
         else:
             i = V.tensor_scalar(out, z, 0.0, 0.05, AluOpType.max, AluOpType.mult)
-        i.then_inc(sem["e%d%d" % (k, b)], 1)
+        i.then_inc(sem["e" + kb], 1)
 
-    def quant_h(k):
+    for n, kb in enumerate(order):
+        if n == 4:
+            inter(S, 3, 256, 512, "bc1")
+        if kb not in VECTOR:
+            relu(S, kb)
+    for w in VECTOR:
+        if len(w) == 2:
+            relu(V, w)
+            continue
+        k = int(w)
         for b in range(4):
             V.wait_ge(sem["e%d%d" % (k, b)], 1)
         V.quantize_mx(T.hq[:, 256 * k:256 * k + 256], T.hp[:, 256 * k:256 * k + 256],
                       T.ht[:, 1024 * k:1024 * k + 1024]).then_inc(sem["qh%d" % k], 1)
 
-    def inter(q, t, a, b, s):
-        out, rows = T.bt[:, 4 * a + t:4 * b:4], T.rw[:, 512 * t + a:512 * t + b]
-        i = S.activation(out, rows, COPY) if q is S else V.tensor_copy(out, rows)
-        i.then_inc(sem[s], 1)
-
-    for b in (0, 2):
-        relu(S, 3, b, b)
-    S.wait_ge(sem.rw3, 16)
-    inter(S, 3, CUT, 256, "bc1")
-    inter(S, 3, 256, 512, "bc2")
-    for k, b, bank in ((2, 0, 0), (2, 2, 2), (0, 1, 1), (1, 3, 3), (0, 3, 1), (1, 1, 3)):
-        relu(S, k, b, bank)
-
-    for t in range(3):
-        V.wait_ge(sem["rw%d" % t], 16)
-        inter(V, t, 0, 512, "bcp")
-    for b in (1, 3):
-        relu(V, 3, b, b)
-    quant_h(3)
-    V.wait_ge(sem.rw3, 16)
-    inter(V, 3, 0, CUT, "bc0")
-    V.wait_ge(sem.bcp, 3)
-    V.wait_ge(sem.bc0, 1)
-    V.wait_ge(sem.bc1, 1)
-    V.quantize_mx(T.bq[:, 0:256], T.bp[:, 0:256], T.bt[:, 0:1024]).then_inc(sem.qb0, 1)
-    V.wait_ge(sem.bc2, 1)
-    V.quantize_mx(T.bq[:, 256:512], T.bp[:, 256:512], T.bt[:, 1024:2048]).then_inc(sem.qb1, 1)
-    for b in (1, 3):
-        relu(V, 2, b, b)
-    quant_h(2)
-    for k, b, bank in ((0, 0, 0), (1, 2, 2), (0, 2, 0), (1, 0, 2)):
-        relu(V, k, b, bank)
-    quant_h(0)
-    quant_h(1)
-
-    def layer1(k, b, bank):
-        w, ws, a = (T.aq, T.ap, 128 * b) if k == 3 else (T.al, T.am, 512 * k + 128 * b)
-        P.matmul_mx(T.ps[:, 512 * bank:512 * bank + 256], w[:, a:a + 128], ws[:, a:a + 128],
-                    T.xq[:], T.xp[:], True, True).then_inc(sem["m%d%d" % (k, b)], 1)
-
-    def layer2(o, k, start, stop):
-        w, ws, a = (T.bq, T.bp, 128 * o) if k == 3 else (T.bl, T.bm, 512 * k + 128 * o)
-        z, c = 2048 + 512 * o, 256 * k
-        i = P.matmul_mx(T.ps[:, z:z + 256], w[:, a:a + 128], ws[:, a:a + 128],
-                        T.hq[:, c:c + 256], T.hp[:, c:c + 256], start, stop)
-        if stop:
-            i.then_inc(sem["ym%d" % o], 1)
+    def stationary(m, k, b):
+        if k == 3:
+            made(P, "%s%d%d" % (m, b, b))
+            return T[m + "q"][:, 128 * b:128 * b + 128], T[m + "p"][:, 128 * b:128 * b + 128]
+        s = slots(me)[k]
+        for i, (lent, direct, near) in enumerate(CALLS):
+            ways = (("c", near, len(shares(s, i)[2])),) if k == 2 else (("c", lent, help_n),
+                                                                        ("d", direct, len(shares(s, i)[1])))
+            for name, pieces, n in ways:
+                if any(p[0].lower() == m and int(p[1]) <= b <= int(p[2]) for p in pieces):
+                    wait(P, "%s%d%d" % (name, i, s), n)
+        a = 512 * k + 128 * b
+        return T[m + "l"][:, a:a + 128], T[m + "m"][:, a:a + 128]
 
     P.wait_ge(sem.xqd, 1)
-    for b in range(4):
-        P.wait_ge(sem["qa%d" % b], 1)
-        layer1(3, b, b)
-    P.wait_ge(sem.qh3, 1)
-    P.wait_ge(sem.qb0, 1)
-    P.wait_ge(sem.qb1, 1)
-    for o in range(4):
-        layer2(o, 3, True, False)
-    for n in ("aa", "as", "ax"):
-        P.wait_ge(sem["%s%d" % (n, nb)], len(near_e))
-    for b in range(4):
-        layer1(2, b, b)
-    for k, r, n, bs in ((0, fa, "aa", (0, 1)), (1, fb, "ax", (2, 3))):
-        P.wait_ge(sem["%s%d" % (n, r)], len(far_e))
-        P.wait_ge(sem["as%d" % r], help_n)
-        for b in bs:
-            P.wait_ge(sem["e2%d" % b], 1)
-            layer1(k, b, b)
-    P.wait_ge(sem["ar%d" % nb], len(near_e))
-    for k, b, bank in ((0, 2, 0), (0, 3, 1), (1, 0, 2), (1, 1, 3)):
-        P.wait_ge(sem["e%d%d" % (bank // 2, bank)], 1)
-        layer1(k, b, bank)
-    P.wait_ge(sem.qh2, 1)
-    for n in ("ab", "bs"):
-        P.wait_ge(sem["%s%d" % (n, nb)], len(near_e))
-    for o in (0, 1):
-        layer2(o, 2, False, False)
-    for k, r in enumerate((fa, fb)):
-        P.wait_ge(sem["qh%d" % k], 1)
-        P.wait_ge(sem["bs%d" % r], len(far_e))
-        P.wait_ge(sem["ab%d" % r], help_n)
-        for o in (0, 1):
-            layer2(o, k, False, k == 1)
-    P.wait_ge(sem["ac%d" % nb], len(near_e))
-    for o in (2, 3):
-        layer2(o, 2, False, False)
-    P.wait_ge(sem["ac%d" % fa], len(far_e))
-    P.wait_ge(sem["ac%d" % fb], len(far_e))
-    for o in (2, 3):
-        layer2(o, 0, False, False)
-        layer2(o, 1, False, True)
+    for n, w in enumerate(TENSOR):
+        k, b = int(w[1]), int(w[2])
+        if w[0] == "1":
+            i = order.index(w[1:])
+            codes, scales = stationary("a", k, b)
+            if i >= 4:
+                P.wait_ge(sem["e" + order[i - 4]], 1)
+            P.matmul_mx(T.ps[:, 512 * (i % 4):512 * (i % 4) + 256], codes, scales,
+                        T.xq[:], T.xp[:], True, True).then_inc(sem["m" + w[1:]], 1)
+        else:
+            group = [j for j, v in enumerate(TENSOR) if v[0] == "2" and v[2] == w[2]]
+            wait(P, "qh%d" % k, 1)
+            codes, scales = stationary("b", k, b)
+            i = P.matmul_mx(T.ps[:, 2048 + 512 * b:2304 + 512 * b], codes, scales, T.hq[:, 256 * k:256 * k + 256],
+                            T.hp[:, 256 * k:256 * k + 256], n == group[0], n == group[-1])
+            if n == group[-1]:
+                i.then_inc(sem["ym%d" % b], 1)
 
-    for o in range(4):
+    ends = sorted(range(4), key=lambda o: max(j for j, v in enumerate(TENSOR) if v[0] == "2" and int(v[2]) == o))
+    for n, o in enumerate(ends):
         a, z = 256 * o, 2048 + 512 * o
-        q = S if o % 2 else V
+        q = S if n in (1, 2) else V
         q.wait_ge(sem["ym%d" % o], 1)
-        if o % 2:
+        if q is S:
             S.activation(T.ys[:, a:a + 256], T.ps[:, z:z + 256], COPY).then_inc(sem["ye%d" % o], 1)
         else:
             V.tensor_copy(T.ys[:, a:a + 256], T.ps[:, z:z + 256]).then_inc(sem["ye%d" % o], 1)
-        Y.wait_ge(sem["ye%d" % o], 1)
-        Y.dma_start(T.y[:, a:a + 256], T.ys[:, a:a + 256]).then_inc(sem.yo, 16)
+        d = S if n == 2 else Y
+        d.wait_ge(sem["ye%d" % o], 1)
+        d.dma_start(T.y[:, a:a + 256], T.ys[:, a:a + 256]).then_inc(sem.yo, 16)
     Y.wait_ge(sem.yo, 64)

@@ -31,23 +31,33 @@ SCRATCH = {
 }
 CALLS = ((("A01",), (), ("A01",)),
          (("a03",), (), ("a03",)),
-         (("A23",), (), ("A23",)),
-         (("B01",), (), ("B01",)),
+         (("A22",), (), ("A22",)),
+         (("A33",), (), ("A33",)),
+         (("B00",), (), ("B00",)),
          (("b03",), (), ("b03",)),
-         ((), ("B22",), ("B22",)),
-         ((), ("B33",), ("B33",)))
+         (("B128:288",), (), ("B128:288",)),
+         (("B33",), (), ("B33",)),
+         ((), ("B288:384",), ("B288:384",)))
 EARLY = (3,)
+STEP = (2, 2)
+SECOND = ()
 GATHER_V, GATHER_S = ((0, 32), (64, 90)), ((32, 64), (90, 128))
-QUANT_A, QUANT_B = ((0, 0), (1, 1), (2, 3)), ((0, 1), (2, 3))
-TENSOR = ("130 131 132 133 120 121 122 123 230 231 232 233 100 101 110 111 102 103 112 113 "
-          "220 221 222 200 201 210 211 202 212 223 203 213").split()
-VECTOR = "3 21 23 2 00 10 02 12 0 1".split()
+QUANT_A, QUANT_B = ("A00", "A11", "A23"), ("B00", "B13")
+TENSOR = ("130 131 132 133 120 121 122 123 230 231 232 233 100 101 110 111 102 112 103 113 "
+          "220 221 223 222 200 210 201 211 202 212 203 213").split()
+VECTOR = "31 33 3 B 21 23 2 00 10 02 03 0 1".split()
 SEMAPHORES = (["actl", "lstl", "xl", "wl", "wg", "xqd", "cp", "dp", "tr", "ofs", "bcp", "sent", "yo"]
-              + ["%s%d" % (n, i) for n in ("gv", "gs", "qa", "qb", "bc", "rw", "ym", "ye", "qh") for i in range(4)]
-              + ["%s%d%d" % (n, i, s) for n in "cd" for i in range(len(CALLS)) for s in range(4)]
+              + ["%s%d" % (n, i) for n in ("gv", "gs", "qa", "qb", "bc", "rw", "ym", "ye", "yf", "qh") for i in range(4)]
+              + ["%s%d%d" % (n, i, s) for i, c in enumerate(CALLS) for n in "cd"[:1 + bool(c[1])] for s in range(4)]
               + ["%s%d%d" % (n, k, b) for n in "me" for k in range(4) for b in range(4)])
 RELU = ActivationFunctionType.Relu
 COPY = ActivationFunctionType.Copy
+
+
+def span(piece):
+    if ":" in piece:
+        return [int(v) for v in piece[1:].split(":")]
+    return 128 * int(piece[1]), 128 * int(piece[2]) + 128
 
 
 def rank_program(g, core, T, topo):
@@ -61,55 +71,56 @@ def rank_program(g, core, T, topo):
         near = [s for s in range(4) if s != r and topo.chip(cores[s]) == topo.chip(c)]
         return off + near + [r]
 
-    def helper(s):
+    def helper(s, piece):
         c = cores[slots(s)[0]]
-        return [h for h in topo.cores_of(c) if topo.die(h) == topo.die(c) and h not in cores][0]
+        return [h for h in topo.cores_of(c) if topo.die(h) == topo.die(c) and h not in cores][piece in SECOND]
 
     def dst(c):
         rid, pid, _ = topo.addr(c)
         return DstId(rid=rid, pnc=pid)
 
     def view(piece, landed, at=0):
-        m, a, b = piece[0], at + 128 * int(piece[1]), at + 128 * int(piece[2]) + 128
+        m, a, b = piece[0], at + span(piece)[0], at + span(piece)[1]
         if m.islower():
             return T[m + ("m" if landed else "p")][:, a:b]
         return T[m.lower() + ("l" if landed else "q")][:, a:b].bitcast(dt.uint8)
 
     def transfers(es, pieces, name, landed, to):
         n = len(es) // max(len(pieces), 1)
-        return [RemoteDMATransfer(dst_ids=[dst(c) for c, _ in to],
+        return [RemoteDMATransfer(dst_ids=[dst(c) for c, _ in to(p)],
                                   dma_engine_mask=sum(1 << e for e in es[n * j:n * j + n]),
                                   remote_sem=sem[name], srcs=[view(p, landed)],
-                                  dsts=[view(p, True, at) for _, at in to]) for j, p in enumerate(pieces)]
+                                  dsts=[view(p, True, at) for _, at in to(p)]) for j, p in enumerate(pieces)]
 
     def place(r, s):
         return cores[r], 512 * slots(r).index(s)
 
     def shares(s, i):
         lent, direct, near = CALLS[i]
-        far = topo.engines(cores[s], helper(s))
+        far = topo.engines(cores[s], cores[slots(s)[0]])
         rest = [e for e in topo.engines(cores[s], cores[slots(s)[2]]) if e not in far]
+        if i < len(EARLY):
+            far, rest = far[::2], rest[::2]
         cut = len(far) // 2 if lent and direct else len(far) * bool(lent)
         return far[:cut], far[cut:] if direct else [], rest if near else []
 
     me = T.rank_of(core)
     if me is None:
         for s in range(4):
-            if helper(s) == core:
+            lent = [(i, p) for i, c in enumerate(CALLS) for p in c[0] if helper(s, p) == core]
+            if lent:
                 rs = slots(s)[:2]
                 es = topo.engines(core, cores[rs[0]])
-                lent = [(i, c[0]) for i, c in enumerate(CALLS) if c[0]]
-                for i, pieces in lent:
+                for i, p in lent:
                     name = "c%d%d" % (i, s)
-                    g.wait_ge(sem[name], len(shares(s, i)[0]))
-                    g.remote_dma_fused([x for j, r in enumerate(rs)
-                                        for x in transfers(es[j::2], pieces, name, True, [place(r, s)])],
-                                       local_sem=sem.sent)
+                    g.wait_ge(sem[name], len(shares(s, i)[0]) // len(CALLS[i][0]))
+                    both = [transfers(es[j::2], [p], name, True, lambda _: [place(r, s)])[0] for j, r in enumerate(rs)]
+                    g.remote_dma_fused(both, local_sem=sem.sent)
                 g.wait_ge(sem.sent, len(lent) * len(es))
         return
 
     fa, fb, nb, _ = slots(me)
-    help_n = len(topo.engines(helper(fa), core)[::2])
+    help_n = len(topo.engines(helper(fa, ""), core)[::2])
     V, S, P, Y = g.vector, g.scalar, g.tensor, g.sync
     waited = []
 
@@ -119,9 +130,9 @@ def rank_program(g, core, T, topo):
             q.wait_ge(sem[name], n)
 
     def made(q, piece):
-        m, a, b = piece[0].lower(), int(piece[1]), int(piece[2])
-        for j, (c, d) in enumerate(QUANT_A if m == "a" else QUANT_B):
-            if c <= b and a <= d:
+        m, (a, b) = piece[0].lower(), span(piece)
+        for j, run in enumerate(QUANT_A if m == "a" else QUANT_B):
+            if span(run)[0] < b and a < span(run)[1]:
                 wait(q, "q%s%d" % (m, j), 1)
 
     def send(i):
@@ -130,16 +141,16 @@ def rank_program(g, core, T, topo):
             made(g, piece)
         to_h, to_far, to_nb = shares(me, i)
         c, d = "c%d%d" % (i, me), "d%d%d" % (i, me)
-        g.remote_dma_fused(transfers(to_h, lent, c, False, [(helper(me), 0)])
-                           + transfers(to_far, direct, d, False, [place(fa, me), place(fb, me)])
-                           + transfers(to_nb, near, c, False, [place(nb, me)]), local_sem=sem.sent)
+        g.remote_dma_fused(transfers(to_h, lent, c, False, lambda p: [(helper(me, p), 0)])
+                           + transfers(to_far, direct, d, False, lambda _: [place(fa, me), place(fb, me)])
+                           + transfers(to_nb, near, c, False, lambda _: [place(nb, me)]), local_sem=sem.sent)
 
     Y.dma_start(T.idx[:], T.act[:]).then_inc(sem.actl, 16)
-    for q, ks, a in ((Y, (0, 1), 0), (S, (2, 3), 2048)):
-        for k in ks:
-            q.dma_start(T.lst[32 * k:32 * k + 32, :], T.act[:]).then_inc(sem.lstl, 16)
-        q.dma_start(T.ws[:, a:a + 2048], T.w1[:, a:a + 2048]).then_inc(sem.wl, 16)
-    g.dma_start(T.ws[:, 4096:6144], T.w1[:, 4096:6144]).then_inc(sem.wg, 16)
+    S.dma_start(T.lst[0:32, :], T.act[:]).then_inc(sem.lstl, 16)
+    for q, a in ((Y, 0), (S, 3072)):
+        q.dma_start(T.ws[16:128, a:a + 3072], T.w1[16:128, a:a + 3072]).then_inc(sem.wl, 16)
+    g.dma_start(T.ws[0:16, :], T.w1[0:16, :]).then_inc(sem.wg, 16)
+    Y.wait_ge(sem.wl, 32)
     Y.dma_start(T.xs[:], T.x[:]).then_inc(sem.xl, 16)
 
     g.wait_ge(sem.actl, 16)
@@ -154,18 +165,19 @@ def rank_program(g, core, T, topo):
         send(i)
     g.wait_ge(sem.sent, sum(len(es) for i in range(len(CALLS)) for es in shares(me, i)))
 
-    V.wait_ge(sem.lstl, 64)
+    V.wait_ge(sem.lstl, 16)
     for b in range(4):
         for t in range(4):
-            V.tensor_scalar(T.lf[:, 32 * b + t:32 * b + 16:4], T.lst[:, b:16:4], 4.0, float(t),
+            V.tensor_scalar(T.lf[0:32, 32 * b + t:32 * b + 16:4], T.lst[0:32, b:16:4], 4.0, float(t),
                             AluOpType.mult, AluOpType.add).then_inc(sem.cp, 1)
     V.wait_ge(sem.cp, 16)
     for b in range(4):
-        V.tensor_copy(T.lf[:, 32 * b + 16:32 * b + 32], T.lf[:, 32 * b:32 * b + 16]).then_inc(sem.dp, 1)
+        V.tensor_copy(T.lf[0:32, 32 * b + 16:32 * b + 32], T.lf[0:32, 32 * b:32 * b + 16]).then_inc(sem.dp, 1)
     V.wait_ge(sem.dp, 4)
-    V.transpose(T.lt[:], T.lf[:]).then_inc(sem.tr, 1)
+    V.transpose(T.lt[0:32, :], T.lf[0:32, :]).then_inc(sem.tr, 1)
     V.wait_ge(sem.tr, 1)
-    V.tensor_copy(T.off[:], T.lt[:]).then_inc(sem.ofs, 1)
+    for k in range(4):
+        V.tensor_copy(T.off[32 * k:32 * k + 32, :], T.lt[0:32, :]).then_inc(sem.ofs, 1)
 
     def gather(q, j):
         a, b = (GATHER_S if q is S else GATHER_V)[j]
@@ -176,14 +188,14 @@ def rank_program(g, core, T, topo):
             V.tensor_copy(out, win).then_inc(sem["gv%d" % j], 1)
 
     for q in (V, S):
-        q.wait_ge(sem.ofs, 1)
+        q.wait_ge(sem.ofs, 4)
         q.wait_ge(sem.wl, 32)
         q.wait_ge(sem.wg, 16)
     for j in range(len(GATHER_S)):
         gather(S, j)
     nxt = 0
-    for j, (c, d) in enumerate(QUANT_A):
-        a, b = 128 * c, 128 * d + 128
+    for j, run in enumerate(QUANT_A):
+        a, b = span(run)
         while nxt < len(GATHER_V) and GATHER_V[nxt][0] < b // 4:
             gather(V, nxt)
             nxt += 1
@@ -203,12 +215,14 @@ def rank_program(g, core, T, topo):
 
     for t in range(3):
         inter(V, t, 0, 512, "bcp")
-    inter(V, 3, 0, 256, "bc0")
-    V.wait_ge(sem.bcp, 3)
-    for j, (c, d) in enumerate(QUANT_B):
-        a, b = 128 * c, 128 * d + 128
-        V.wait_ge(sem["bc%d" % j], 1)
-        V.quantize_mx(T.bq[:, a:b], T.bp[:, a:b], T.bt[:, 4 * a:4 * b]).then_inc(sem["qb%d" % j], 1)
+
+    def finish_b():
+        inter(V, 3, 0, 256, "bc0")
+        V.wait_ge(sem.bcp, 3)
+        for j, run in enumerate(QUANT_B):
+            a, b = span(run)
+            wait(V, "bc%d" % ((b - 1) // 256), 1)
+            V.quantize_mx(T.bq[:, a:b], T.bp[:, a:b], T.bt[:, 4 * a:4 * b]).then_inc(sem["qb%d" % j], 1)
 
     order = [w[1:] for w in TENSOR if w[0] == "1"]
 
@@ -231,6 +245,9 @@ def rank_program(g, core, T, topo):
         if len(w) == 2:
             relu(V, w)
             continue
+        if w == "B":
+            finish_b()
+            continue
         k = int(w)
         for b in range(4):
             V.wait_ge(sem["e%d%d" % (k, b)], 1)
@@ -243,10 +260,10 @@ def rank_program(g, core, T, topo):
             return T[m + "q"][:, 128 * b:128 * b + 128], T[m + "p"][:, 128 * b:128 * b + 128]
         s = slots(me)[k]
         for i, (lent, direct, near) in enumerate(CALLS):
-            ways = (("c", near, len(shares(s, i)[2])),) if k == 2 else (("c", lent, help_n),
+            ways = (("c", near, len(shares(s, i)[2])),) if k == 2 else (("c", lent, help_n * len(lent)),
                                                                         ("d", direct, len(shares(s, i)[1])))
             for name, pieces, n in ways:
-                if any(p[0].lower() == m and int(p[1]) <= b <= int(p[2]) for p in pieces):
+                if any(p[0].lower() == m and span(p)[0] < 128 * b + 128 and 128 * b < span(p)[1] for p in pieces):
                     wait(P, "%s%d%d" % (name, i, s), n)
         a = 512 * k + 128 * b
         return T[m + "l"][:, a:a + 128], T[m + "m"][:, a:a + 128]
@@ -273,13 +290,12 @@ def rank_program(g, core, T, topo):
     ends = sorted(range(4), key=lambda o: max(j for j, v in enumerate(TENSOR) if v[0] == "2" and int(v[2]) == o))
     for n, o in enumerate(ends):
         a, z = 256 * o, 2048 + 512 * o
-        q = S if n in (1, 2) else V
+        q = S if n == 1 else V
         q.wait_ge(sem["ym%d" % o], 1)
-        if q is S:
-            S.activation(T.ys[:, a:a + 256], T.ps[:, z:z + 256], COPY).then_inc(sem["ye%d" % o], 1)
-        else:
-            V.tensor_copy(T.ys[:, a:a + 256], T.ps[:, z:z + 256]).then_inc(sem["ye%d" % o], 1)
-        d = S if n == 2 else Y
+        out, part = T.ys[:, a:a + 256], T.ps[:, z:z + 256]
+        i = S.activation(out, part, COPY) if q is S else V.tensor_copy(out, part)
+        i.then_inc(sem["ye%d" % o], 1)
+        d = S if n % 2 else Y
         d.wait_ge(sem["ye%d" % o], 1)
-        d.dma_start(T.y[:, a:a + 256], T.ys[:, a:a + 256]).then_inc(sem.yo, 16)
+        d.dma_start(T.y[:, a:a + 256], out).then_inc(sem.yo, 16)
     Y.wait_ge(sem.yo, 64)

from concourse.bass import DstId, RemoteDMATransfer, IndirectOffsetOnAxis
from concourse.mybir import dt, AluOpType, ActivationFunctionType

F8 = "float8_e4m3fn_x4"
SCRATCH = {
    "idx": ("sbuf", [128, 4], "int32"),
    "lst": ("sbuf", [128, 16], "int32"),
    "lf": ("sbuf", [128, 128], "float32"),
    "lt": ("sbuf", [128, 128], "float32"),
    "off": ("sbuf", [128, 128], "uint16"),
    "xs": ("sbuf", [128, 1024], "bfloat16"),
    "xq": ("sbuf", [128, 256], F8),
    "xp": ("sbuf", [128, 256], "uint8"),
    "ws": ("sbuf", [128, 6144], "bfloat16"),
    "at": ("sbuf", [128, 2048], "bfloat16"),
    "aq": ("sbuf", [128, 512], F8),
    "ap": ("sbuf", [128, 512], "uint8"),
    "rw": ("sbuf", [128, 2048], "bfloat16"),
    "bt": ("sbuf", [128, 2048], "bfloat16"),
    "bq": ("sbuf", [128, 512], F8),
    "bp": ("sbuf", [128, 512], "uint8"),
    "al": ("sbuf", [128, 1536], F8),
    "am": ("sbuf", [128, 1536], "uint8"),
    "bl": ("sbuf", [128, 1536], F8),
    "bm": ("sbuf", [128, 1536], "uint8"),
    "ht": ("sbuf", [128, 4096], "bfloat16"),
    "hq": ("sbuf", [128, 1024], F8),
    "hp": ("sbuf", [128, 1024], "uint8"),
    "ys": ("sbuf", [128, 1024], "float32"),
    "ps": ("psum", [128, 4096], "float32"),
}
CALLS = ((("A01",), (), ("A01",)),
         (("a03",), (), ("a03",)),
         (("A22",), (), ("A22",)),
         (("A33",), (), ("A33",)),
         (("B00",), (), ("B00",)),
         (("b03",), (), ("b03",)),
         (("B128:288",), (), ("B128:288",)),
         (("B33",), (), ("B33",)),
         ((), ("B288:384",), ("B288:384",)))
EARLY = (3,)
STEP = (2, 2)
SECOND = ()
GATHER_V, GATHER_S = ((0, 32), (64, 90)), ((32, 64), (90, 128))
QUANT_A, QUANT_B = ("A00", "A11", "A23"), ("B00", "B13")
TENSOR = ("130 131 132 133 120 121 122 123 230 231 232 233 100 101 110 111 102 112 103 113 "
          "220 221 223 222 200 210 201 211 202 212 203 213").split()
VECTOR = "31 33 3 B 21 23 2 00 10 02 03 0 1".split()
SEMAPHORES = (["actl", "lstl", "xl", "wl", "wg", "xqd", "cp", "dp", "tr", "ofs", "bcp", "sent", "yo"]
              + ["%s%d" % (n, i) for n in ("gv", "gs", "qa", "qb", "bc", "rw", "ym", "ye", "yf", "qh") for i in range(4)]
              + ["%s%d%d" % (n, i, s) for i, c in enumerate(CALLS) for n in "cd"[:1 + bool(c[1])] for s in range(4)]
              + ["%s%d%d" % (n, k, b) for n in "me" for k in range(4) for b in range(4)])
RELU = ActivationFunctionType.Relu
COPY = ActivationFunctionType.Copy


def span(piece):
    if ":" in piece:
        return [int(v) for v in piece[1:].split(":")]
    return 128 * int(piece[1]), 128 * int(piece[2]) + 128


def rank_program(g, core, T, topo):
    cores = T.cores
    sem = T.sem

    def slots(r):
        c = cores[r]
        off = [s for s in range(4) if topo.chip(cores[s]) != topo.chip(c)]
        off.sort(key=lambda s: topo.die(cores[s]) != topo.die(c))
        near = [s for s in range(4) if s != r and topo.chip(cores[s]) == topo.chip(c)]
        return off + near + [r]

    def helper(s, piece):
        c = cores[slots(s)[0]]
        return [h for h in topo.cores_of(c) if topo.die(h) == topo.die(c) and h not in cores][piece in SECOND]

    def dst(c):
        rid, pid, _ = topo.addr(c)
        return DstId(rid=rid, pnc=pid)

    def view(piece, landed, at=0):
        m, a, b = piece[0], at + span(piece)[0], at + span(piece)[1]
        if m.islower():
            return T[m + ("m" if landed else "p")][:, a:b]
        return T[m.lower() + ("l" if landed else "q")][:, a:b].bitcast(dt.uint8)

    def transfers(es, pieces, name, landed, to):
        n = len(es) // max(len(pieces), 1)
        return [RemoteDMATransfer(dst_ids=[dst(c) for c, _ in to(p)],
                                  dma_engine_mask=sum(1 << e for e in es[n * j:n * j + n]),
                                  remote_sem=sem[name], srcs=[view(p, landed)],
                                  dsts=[view(p, True, at) for _, at in to(p)]) for j, p in enumerate(pieces)]

    def place(r, s):
        return cores[r], 512 * slots(r).index(s)

    def shares(s, i):
        lent, direct, near = CALLS[i]
        far = topo.engines(cores[s], cores[slots(s)[0]])
        rest = [e for e in topo.engines(cores[s], cores[slots(s)[2]]) if e not in far]
        if i < len(EARLY):
            far, rest = far[::2], rest[::2]
        cut = len(far) // 2 if lent and direct else len(far) * bool(lent)
        return far[:cut], far[cut:] if direct else [], rest if near else []

    me = T.rank_of(core)
    if me is None:
        for s in range(4):
            lent = [(i, p) for i, c in enumerate(CALLS) for p in c[0] if helper(s, p) == core]
            if lent:
                rs = slots(s)[:2]
                es = topo.engines(core, cores[rs[0]])
                for i, p in lent:
                    name = "c%d%d" % (i, s)
                    g.wait_ge(sem[name], len(shares(s, i)[0]) // len(CALLS[i][0]))
                    both = [transfers(es[j::2], [p], name, True, lambda _: [place(r, s)])[0] for j, r in enumerate(rs)]
                    g.remote_dma_fused(both, local_sem=sem.sent)
                g.wait_ge(sem.sent, len(lent) * len(es))
        return

    fa, fb, nb, _ = slots(me)
    help_n = len(topo.engines(helper(fa, ""), core)[::2])
    V, S, P, Y = g.vector, g.scalar, g.tensor, g.sync
    waited = []

    def wait(q, name, n):
        if not any(w[0] is q and w[1] == name for w in waited):
            waited.append((q, name))
            q.wait_ge(sem[name], n)

    def made(q, piece):
        m, (a, b) = piece[0].lower(), span(piece)
        for j, run in enumerate(QUANT_A if m == "a" else QUANT_B):
            if span(run)[0] < b and a < span(run)[1]:
                wait(q, "q%s%d" % (m, j), 1)

    def send(i):
        lent, direct, near = CALLS[i]
        for piece in lent + direct + near:
            made(g, piece)
        to_h, to_far, to_nb = shares(me, i)
        c, d = "c%d%d" % (i, me), "d%d%d" % (i, me)
        g.remote_dma_fused(transfers(to_h, lent, c, False, lambda p: [(helper(me, p), 0)])
                           + transfers(to_far, direct, d, False, lambda _: [place(fa, me), place(fb, me)])
                           + transfers(to_nb, near, c, False, lambda _: [place(nb, me)]), local_sem=sem.sent)

    Y.dma_start(T.idx[:], T.act[:]).then_inc(sem.actl, 16)
    S.dma_start(T.lst[0:32, :], T.act[:]).then_inc(sem.lstl, 16)
    for q, a in ((Y, 0), (S, 3072)):
        q.dma_start(T.ws[16:128, a:a + 3072], T.w1[16:128, a:a + 3072]).then_inc(sem.wl, 16)
    g.dma_start(T.ws[0:16, :], T.w1[0:16, :]).then_inc(sem.wg, 16)
    Y.wait_ge(sem.wl, 32)
    Y.dma_start(T.xs[:], T.x[:]).then_inc(sem.xl, 16)

    g.wait_ge(sem.actl, 16)
    for t in range(4):
        for i in range(len(EARLY)):
            if EARLY[i] == t:
                send(i)
        g.indirect_dma_start(T.rw[:, 512 * t:512 * t + 512], None, T.w2[:],
                             IndirectOffsetOnAxis(ap=T.idx[:, t:t + 1], axis=0),
                             bounds_check=1535).then_inc(sem["rw%d" % t], 16)
    for i in range(len(EARLY), len(CALLS)):
        send(i)
    g.wait_ge(sem.sent, sum(len(es) for i in range(len(CALLS)) for es in shares(me, i)))

    V.wait_ge(sem.lstl, 16)
    for b in range(4):
        for t in range(4):
            V.tensor_scalar(T.lf[0:32, 32 * b + t:32 * b + 16:4], T.lst[0:32, b:16:4], 4.0, float(t),
                            AluOpType.mult, AluOpType.add).then_inc(sem.cp, 1)
    V.wait_ge(sem.cp, 16)
    for b in range(4):
        V.tensor_copy(T.lf[0:32, 32 * b + 16:32 * b + 32], T.lf[0:32, 32 * b:32 * b + 16]).then_inc(sem.dp, 1)
    V.wait_ge(sem.dp, 4)
    V.transpose(T.lt[0:32, :], T.lf[0:32, :]).then_inc(sem.tr, 1)
    V.wait_ge(sem.tr, 1)
    for k in range(4):
        V.tensor_copy(T.off[32 * k:32 * k + 32, :], T.lt[0:32, :]).then_inc(sem.ofs, 1)

    def gather(q, j):
        a, b = (GATHER_S if q is S else GATHER_V)[j]
        out, win = T.at[:, 16 * a:16 * b], T.ws[:, 0:6144].indirect(T.off[:, a:b])
        if q is S:
            S.activation(out, win, COPY).then_inc(sem["gs%d" % j], 1)
        else:
            V.tensor_copy(out, win).then_inc(sem["gv%d" % j], 1)

    for q in (V, S):
        q.wait_ge(sem.ofs, 4)
        q.wait_ge(sem.wl, 32)
        q.wait_ge(sem.wg, 16)
    for j in range(len(GATHER_S)):
        gather(S, j)
    nxt = 0
    for j, run in enumerate(QUANT_A):
        a, b = span(run)
        while nxt < len(GATHER_V) and GATHER_V[nxt][0] < b // 4:
            gather(V, nxt)
            nxt += 1
        for name, runs in (("gv", GATHER_V), ("gs", GATHER_S)):
            for i, (u, v) in enumerate(runs):
                if u < b // 4 and a // 4 < v:
                    wait(V, "%s%d" % (name, i), 1)
        V.quantize_mx(T.aq[:, a:b], T.ap[:, a:b], T.at[:, 4 * a:4 * b]).then_inc(sem["qa%d" % j], 1)
    V.wait_ge(sem.xl, 16)
    V.quantize_mx(T.xq[:], T.xp[:], T.xs[:]).then_inc(sem.xqd, 1)

    def inter(q, t, a, b, s):
        out, rows = T.bt[:, 4 * a + t:4 * b:4], T.rw[:, 512 * t + a:512 * t + b]
        q.wait_ge(sem["rw%d" % t], 16)
        i = S.activation(out, rows, COPY) if q is S else V.tensor_copy(out, rows)
        i.then_inc(sem[s], 1)

    for t in range(3):
        inter(V, t, 0, 512, "bcp")

    def finish_b():
        inter(V, 3, 0, 256, "bc0")
        V.wait_ge(sem.bcp, 3)
        for j, run in enumerate(QUANT_B):
            a, b = span(run)
            wait(V, "bc%d" % ((b - 1) // 256), 1)
            V.quantize_mx(T.bq[:, a:b], T.bp[:, a:b], T.bt[:, 4 * a:4 * b]).then_inc(sem["qb%d" % j], 1)

    order = [w[1:] for w in TENSOR if w[0] == "1"]

    def relu(q, kb):
        k, b, bank = int(kb[0]), int(kb[1]), order.index(kb) % 4
        q.wait_ge(sem["m" + kb], 1)
        out, z = T.ht[:, 1024 * k + b:1024 * k + 1024:4], T.ps[:, 512 * bank:512 * bank + 256]
        if q is S:
            i = S.activation(out, z, RELU, scale=0.05)
        else:
            i = V.tensor_scalar(out, z, 0.0, 0.05, AluOpType.max, AluOpType.mult)
        i.then_inc(sem["e" + kb], 1)

    for n, kb in enumerate(order):
        if n == 4:
            inter(S, 3, 256, 512, "bc1")
        if kb not in VECTOR:
            relu(S, kb)
    for w in VECTOR:
        if len(w) == 2:
            relu(V, w)
            continue
        if w == "B":
            finish_b()
            continue
        k = int(w)
        for b in range(4):
            V.wait_ge(sem["e%d%d" % (k, b)], 1)
        V.quantize_mx(T.hq[:, 256 * k:256 * k + 256], T.hp[:, 256 * k:256 * k + 256],
                      T.ht[:, 1024 * k:1024 * k + 1024]).then_inc(sem["qh%d" % k], 1)

    def stationary(m, k, b):
        if k == 3:
            made(P, "%s%d%d" % (m, b, b))
            return T[m + "q"][:, 128 * b:128 * b + 128], T[m + "p"][:, 128 * b:128 * b + 128]
        s = slots(me)[k]
        for i, (lent, direct, near) in enumerate(CALLS):
            ways = (("c", near, len(shares(s, i)[2])),) if k == 2 else (("c", lent, help_n * len(lent)),
                                                                        ("d", direct, len(shares(s, i)[1])))
            for name, pieces, n in ways:
                if any(p[0].lower() == m and span(p)[0] < 128 * b + 128 and 128 * b < span(p)[1] for p in pieces):
                    wait(P, "%s%d%d" % (name, i, s), n)
        a = 512 * k + 128 * b
        return T[m + "l"][:, a:a + 128], T[m + "m"][:, a:a + 128]

    P.wait_ge(sem.xqd, 1)
    for n, w in enumerate(TENSOR):
        k, b = int(w[1]), int(w[2])
        if w[0] == "1":
            i = order.index(w[1:])
            codes, scales = stationary("a", k, b)
            if i >= 4:
                P.wait_ge(sem["e" + order[i - 4]], 1)
            P.matmul_mx(T.ps[:, 512 * (i % 4):512 * (i % 4) + 256], codes, scales,
                        T.xq[:], T.xp[:], True, True).then_inc(sem["m" + w[1:]], 1)
        else:
            group = [j for j, v in enumerate(TENSOR) if v[0] == "2" and v[2] == w[2]]
            wait(P, "qh%d" % k, 1)
            codes, scales = stationary("b", k, b)
            i = P.matmul_mx(T.ps[:, 2048 + 512 * b:2304 + 512 * b], codes, scales, T.hq[:, 256 * k:256 * k + 256],
                            T.hp[:, 256 * k:256 * k + 256], n == group[0], n == group[-1])
            if n == group[-1]:
                i.then_inc(sem["ym%d" % b], 1)

    ends = sorted(range(4), key=lambda o: max(j for j, v in enumerate(TENSOR) if v[0] == "2" and int(v[2]) == o))
    for n, o in enumerate(ends):
        a, z = 256 * o, 2048 + 512 * o
        q = S if n == 1 else V
        q.wait_ge(sem["ym%d" % o], 1)
        out, part = T.ys[:, a:a + 256], T.ps[:, z:z + 256]
        i = S.activation(out, part, COPY) if q is S else V.tensor_copy(out, part)
        i.then_inc(sem["ye%d" % o], 1)
        d = S if n % 2 else Y
        d.wait_ge(sem["ye%d" % o], 1)
        d.dma_start(T.y[:, a:a + 256], out).then_inc(sem.yo, 16)
    Y.wait_ge(sem.yo, 64)
